import numpy as np
import ml_dtypes


def mxq(x, axis, fmt="e4m3"):
    dtype, down = {"e4m3": (ml_dtypes.float8_e4m3fn, 7), "e5m2": (ml_dtypes.float8_e5m2, 14)}[fmt]
    v = np.moveaxis(np.asarray(x, np.float32).astype(ml_dtypes.bfloat16).astype(np.float64), axis, -1)
    blocks = v.reshape(v.shape[:-1] + (-1, 32))
    amax = np.abs(blocks).max(-1, keepdims=True)
    byte = np.maximum(np.where(amax > 0, np.frexp(amax)[1] - 1 + 127, 0) - down, 1)
    scale = np.exp2(byte - 127.0)
    codes = (blocks / scale).astype(np.float32).astype(dtype).astype(np.float64)
    return np.moveaxis((codes * scale).reshape(v.shape), -1, axis)


WIDE = False


def mx_kscale(k):
    if not WIDE:
        return np.ones(k)
    levels = np.array([10, -10, 5, -5, 0])
    if k % 512:
        return np.exp2(np.random.permutation(np.resize(levels, k // 32))).repeat(32)
    a = np.empty((k // 512, 16))
    for p in range(k // 512):
        a[p, :8] = np.random.permutation(np.resize(levels, 8))
        for g in range(8):
            far = levels[np.abs(levels - a[p, g]) >= 10]
            a[p, g + 8] = far[np.random.randint(len(far))]
    return np.exp2(a.ravel()).repeat(32)


def f64(x):
    return np.asarray(x).astype(np.float64)


def striped(idx):
    return np.tile(idx.reshape(-1, 16).T, (8, 1)).astype(np.uint16)


def unstriped(offs):
    return offs[:16].T.reshape(-1).astype(np.int64)


def pack_weight(w):
    k, n = w.shape
    w = f64(np.asarray(w, np.float32).astype(ml_dtypes.bfloat16)).reshape(k // 32, 32, n)
    amax = np.abs(w).max(1)
    byte = np.clip(np.where(amax > 0, np.frexp(amax)[1] - 1 + 127 - 7, 1), 1, 254)
    scaled = (w * np.exp2(127.0 - byte)[:, None, :]).reshape(k, n).astype(np.float32)
    words = np.ascontiguousarray(scaled.reshape(k // 512, 128, 4, n).transpose(0, 1, 3, 2)).astype(ml_dtypes.float8_e4m3fn).view(np.uint8)
    return words, np.ascontiguousarray(byte.astype(np.uint8).reshape(k // 512, 16, n))


def unpack_weight(words, scales):
    g, p, n, _ = words.shape
    vals = np.ascontiguousarray(words).view(ml_dtypes.float8_e4m3fn).astype(np.float64) * np.repeat(np.exp2(scales.astype(np.float64) - 127.0), 8, axis=1)[..., None]
    return vals.transpose(0, 1, 3, 2).reshape(g * 512, n)


K, T, S, D, N, H = 1024, 2048, 512, 4, 128, 512


def setup_inputs():
    n = np.random.standard_normal
    s = mx_kscale(K)[:, None]
    u = mx_kscale(H)
    packed_xT = pack_weight(n((K, T)) * s)
    return {
        "x_words": packed_xT[0],
        "x_scales": packed_xT[1],
        "w1": (n((K, H)) / np.sqrt(K) / s).astype(np.float32),
        "w2": (n((K, H)) / np.sqrt(K) / s).astype(np.float32),
        "beta": (np.random.uniform(0.6, 1.2, (H, 1))).astype(np.float32),
        "unit": (np.random.uniform(0.6, 1.4, (H, 1)) * u[:, None]).astype(np.float32),
        "w3": (n((H, N)) / np.sqrt(H) / u[:, None]).astype(np.float32),
        "offs": striped(np.random.permutation(T)[:S]),
        "nei": striped(np.random.permutation(S)),
    }


def reference(x_words, x_scales, w1, w2, beta, unit, w3, offs, nei):
    xq = unpack_weight(x_words, x_scales)[:, unstriped(offs)]
    un = mxq(f64(w1), 0, "e4m3").T @ xq
    sp = mxq(f64(w2), 0, "e4m3").T @ xq
    vel = f64(beta) * (np.log(np.exp(un) + 1.0)) - (0.7 * (np.log(np.exp(sp) + 1.0)))
    sn = sp[:, unstriped(nei)]
    dst = sn - sp
    cosn = (vel * dst) / (np.abs(vel) + np.abs(dst) + 0.3)
    prtop = cosn.reshape(len(cosn), -1, D).max(axis=2)
    prexp = np.exp(cosn - np.repeat(prtop, D, axis=1))
    prsum = prexp.reshape(len(prexp), -1, D).sum(axis=2)
    pr = prexp / np.repeat(prsum, D, axis=1)
    drft = pr * dst
    hid = f64(unit) * (drft - (0.4 * vel))
    return mxq(f64(w3), 0, "e4m3").T @ mxq(hid, 0, "e4m3")

from contextlib import ExitStack

import concourse.mybir as mybir
from concourse.masks import make_identity

K, T, S, D, N, H = 1024, 2048, 512, 4, 128, 512
FLOPS = 2 * (2 * K * H * S + H * N * S)

F32 = mybir.dt.float32
BF16 = mybir.dt.bfloat16
I32 = mybir.dt.int32
U32 = mybir.dt.uint32
U16 = mybir.dt.uint16
U8 = mybir.dt.uint8
FP8X4 = mybir.dt.float8_e4m3fn_x4
ACT = mybir.ActivationFunctionType
ALU = mybir.AluOpType
AXIS_X = mybir.AxisListType.X

P = 128
PACK = 4
PASSES = K // (P * PACK)
HALF = S // 2
STRIPS = 4
RUN = 32
CUT = 64
GROUPS = S // D
TINY = 1e-18


def tile_picked_yrnavl_drift_p_kernel(
    tc, x_words, x_scales, w1, w2, beta, unit, w3, offs, nei, out
):
    nc = tc.nc
    with ExitStack() as ctx:
        keep = ctx.enter_context(tc.tile_pool(name="keep", bufs=1))
        psum = ctx.enter_context(tc.psum_pool(name="psum", bufs=1))

        def sb(name, shape, dtype):
            return keep.tile(shape, dtype, name=name, align_bytes=64)

        offs_sb = keep.tile([P, S // 16], U16, name="offs_sb")
        nei_sb = keep.tile([P, S // 16], U16, name="nei_sb")

        x_table = [sb("x_table%d" % o, [P, T], I32) for o in range(PASSES)]
        x_scale_table = sb("x_scale_table", [P, T // 4], I32)
        x_codes = [sb("x_codes%d" % o, [P, S], I32) for o in range(PASSES)]
        x_scale = sb("x_scale", [P, S], U8)

        def load_rows(name, w, o, c0, c1):
            raw = sb(name, [P, PACK, c1 - c0], F32)
            rows = w[o * P * PACK : (o + 1) * P * PACK, c0:c1]
            nc.sync.dma_start(out=raw[:], in_=rows.rearrange("(p j) c -> p j c", j=PACK))
            return raw

        def load_x(o):
            nc.sync.dma_start(out=x_table[o][:], in_=x_words[o].rearrange("p n r -> p (n r)").bitcast(I32))

        nc.sync.dma_start(offs_sb[:], offs)
        nc.vector.memset(x_scale_table[:], 0)
        for q in range(4):
            nc.scalar.dma_start(
                out=x_scale_table[32 * q : 32 * q + 4 * PASSES, :],
                in_=x_scales[:, 4 * q : 4 * q + 4, :].bitcast(I32),
            )
        w2_raw = []
        for o in range(PASSES):
            w2_raw.append(load_rows("w2_raw%d" % o, w2, o, 0, H))
            load_x(o)
        nc.sync.dma_start(nei_sb[:], nei)
        w1_raw = [
            [load_rows("w1_raw%d_%d" % (o, h), w1, o, h * H // 2, (h + 1) * H // 2) for h in range(2)]
            for o in range(PASSES)
        ]
        w3_raw = sb("w3_raw", [P, PACK, N], F32)
        nc.sync.dma_start(out=w3_raw[:], in_=w3.rearrange("(p j) n -> p j n", j=PACK))
        beta_sb = sb("beta_sb", [P, PACK], F32)
        unit_sb = sb("unit_sb", [P, PACK], F32)
        nc.scalar.dma_start(out=beta_sb[:], in_=beta.rearrange("(p t) o -> p (t o)", t=PACK))
        nc.scalar.dma_start(out=unit_sb[:], in_=unit.rearrange("(p t) o -> p (t o)", t=PACK))

        def deal(copy, grouped, m0, raw_cols):
            count = raw_cols.shape[2] // PACK
            copy(
                out=grouped[:, :, m0 : m0 + count, :].rearrange("p t m j -> p m j t"),
                in_=raw_cols.rearrange("p j (m t) -> p m j t", t=PACK),
            )

        def quantize(name, values, width):
            codes = sb(name + "_codes", [P, width], I32)
            scale = sb(name + "_scale", [P, width], U8)
            nc.vector.quantize_mx(out=codes[:].bitcast(FP8X4), scales=scale[:], in_=values)
            return codes, scale

        def product(bank, w_q, t):
            cols = slice(t * P, (t + 1) * P)
            for o in range(PASSES):
                nc.tensor.matmul_mx(
                    out=bank[:],
                    lhsT=w_q[o][0][:, cols].bitcast(FP8X4),
                    lhsT_scale=w_q[o][1][:, cols],
                    rhs=x_codes[o][:].bitcast(FP8X4),
                    rhs_scale=x_scale[4 * o : P, :],
                    start=(o == 0),
                    stop=(o == PASSES - 1),
                )

        identity = sb("identity", [P, P], F32)
        make_identity(nc, identity[:])

        w2_q = []
        for o in range(PASSES):
            grouped = sb("w2_grouped%d" % o, [P, PACK, P, PACK], BF16)
            deal(nc.vector.tensor_copy, grouped, 0, w2_raw[o][:, :, 0 : H // 2])
            deal(nc.scalar.copy, grouped, P // 2, w2_raw[o][:, :, H // 2 : H])
            w2_q.append(quantize("w2_%d" % o, grouped[:].rearrange("p t m j -> p (t m j)"), H))
            nc.vector.tensor_copy(x_codes[o][:].bitcast(U32), x_table[o][:].bitcast(U32).indirect(offs_sb[:]))
            if o == 0:
                nc.vector.tensor_copy(x_scale[:], x_scale_table[:].bitcast(U8).indirect(offs_sb[:]))

        sp_bank = [psum.tile([P, S], F32, name="sp_bank%d" % t, tag="a%d" % t) for t in range(PACK)]
        un_bank = [psum.tile([P, S], F32, name="un_bank%d" % t, tag="b%d" % t) for t in range(PACK)]
        for t in range(PACK):
            product(sp_bank[t], w2_q, t)

        sig = sb("sig", [P, 2 * PACK, S], F32)
        sp_window = [sb("sp_window%d" % t, [P, S], F32) for t in range(PACK)]
        sp = sb("sp", [P, PACK, S], F32)
        dst = sb("dst", [P, PACK, S], F32)
        for t in range(PACK):
            nc.scalar.activation(sig[:, t, :], sp_bank[t][:], ACT.Sigmoid, scale=-1.0)
            nc.scalar.copy(sp_window[t][:], sp_bank[t][:])
            nc.sync.dma_start(out=sp[:, t, :], in_=sp_window[t][:])

        w1_q = []
        for o in range(PASSES):
            grouped = sb("w1_grouped%d" % o, [P, PACK, P, PACK], BF16)
            for h in range(2):
                deal(nc.vector.tensor_copy, grouped, h * P // 2, w1_raw[o][h][:])
            if o < PASSES - 1:
                w1_q.append(quantize("w1_%d" % o, grouped[:].rearrange("p t m j -> p (t m j)"), H))
            else:
                codes = sb("w1_last_codes", [P, H], I32)
                scale = sb("w1_last_scale", [P, H], U8)
                for t in range(PACK):
                    nc.vector.quantize_mx(
                        out=codes[:, t * P : (t + 1) * P].bitcast(FP8X4),
                        scales=scale[:, t * P : (t + 1) * P],
                        in_=grouped[:, t, :, :].rearrange("p m j -> p (m j)"),
                    )
                w1_q.append((codes, scale))
        for t in range(PACK):
            product(un_bank[t], w1_q, t)
        for t in range(PACK):
            nc.scalar.activation(sig[:, PACK + t, :], un_bank[t][:], ACT.Sigmoid, scale=-1.0)

        beta_f = sb("beta_f", [P, PACK], F32)
        unit_f = sb("unit_f", [P, PACK], F32)
        nc.gpsimd.tensor_scalar(beta_f[:], beta_sb[:], -1.0 / 0.7, 0.0, ALU.mult, ALU.add)
        nc.gpsimd.tensor_scalar(unit_f[:], unit_sb[:], -0.4 * 0.7, 0.0, ALU.mult, ALU.add)

        for t in range(PACK):
            for c in range(2):
                cols = slice(c * HALF, (c + 1) * HALF)
                picks = nei_sb[:, c * HALF // 16 : (c + 1) * HALF // 16]
                nc.vector.tensor_tensor(dst[:, t, cols], sp_window[t][:].indirect(picks), sp[:, t, cols], ALU.subtract)

        def half(rows, c):
            return rows.rearrange("p t (s c j) -> p (t s) c j", c=2, j=CUT)[:, :, c, :]

        def cuts(rows):
            return rows.rearrange("p t (s j) -> p (t s) j", j=CUT)

        abs_dst = sig[:, 0:PACK, :]
        log_den = sig[:, PACK : 2 * PACK, :]
        vel = sb("vel", [P, PACK, S], F32)
        log_sig = []
        for c in range(2):
            piece = sb("log_sig%d" % c, [P, 2 * PACK, HALF], F32)
            nc.scalar.activation(cuts(piece[:]), half(sig[:], c), ACT.Ln, bias=TINY)
            log_sig.append(piece)
        for t in range(PACK):
            nc.scalar.activation(abs_dst[:, t, :], dst[:, t, :], ACT.Abs)
        for c in range(2):
            neg_s = log_sig[c][:, 0:PACK, :]
            neg_u = log_sig[c][:, PACK : 2 * PACK, :]
            den = sb("den%d" % c, [P, PACK, HALF], F32)
            nc.vector.scalar_tensor_tensor(cuts(neg_s), half(sp[:], c), -1.0, cuts(neg_s), ALU.mult, ALU.min)
            for pair in range(2):
                tiles = slice(2 * pair, 2 * pair + 2)
                for t in range(2 * pair, 2 * pair + 2):
                    rows = cuts(neg_u[:, t : t + 1, :])
                    nc.vector.scalar_tensor_tensor(
                        rows, half(un_bank[t][:].unsqueeze(1), c), -1.0, rows, ALU.mult, ALU.min
                    )
                for t in range(2 * pair, 2 * pair + 2):
                    nc.vector.scalar_tensor_tensor(
                        half(vel[:, t : t + 1, :], c),
                        cuts(neg_u[:, t : t + 1, :]),
                        beta_f[:, t : t + 1],
                        cuts(neg_s[:, t : t + 1, :]),
                        ALU.mult,
                        ALU.add,
                    )
                nc.scalar.activation(cuts(den[:, tiles, :]), half(vel[:, tiles, :], c), ACT.Abs, scale=0.7)
            for pair in range(2):
                tiles = slice(2 * pair, 2 * pair + 2)
                rows = cuts(den[:, tiles, :])
                nc.vector.tensor_tensor(rows, rows, half(abs_dst[:, tiles, :], c), ALU.add)
                nc.scalar.activation(half(log_den[:, tiles, :], c), rows, ACT.Ln, bias=0.3)

        def members(rows):
            return rows.rearrange("p (v d) -> p v d", d=D)

        num = sb("num", [P, D, PACK, GROUPS], F32)
        for t in range(PACK):
            nc.vector.scalar_tensor_tensor(
                num[:, :, t, :].rearrange("p d v -> p v d"),
                members(vel[:, t, :]),
                0.7,
                members(dst[:, t, :]),
                ALU.mult,
                ALU.mult,
            )

        slots = sb("slots", [P, PACK + 1, S], F32)
        unit_dst = slots[:, 0:PACK, :].rearrange("p t (d v) -> p t d v", d=D)
        unit_vel = num[:].rearrange("p d t v -> p (d t v)").rearrange("p (s t d v) -> p s t d v", s=STRIPS, t=PACK, d=D)
        cosn = [sb("cosn%d" % k, [P, D, PACK, RUN], F32) for k in range(STRIPS)]
        for k in range(STRIPS):
            nc.scalar.activation(
                cosn[k][:].rearrange("p d t v -> p t v d"),
                log_den[:, :, k * P : (k + 1) * P].rearrange("p t (v d) -> p t v d", d=D),
                ACT.Exp,
                scale=-1.0,
            )
        sum_bank = psum.tile([P, STRIPS, P], F32, name="sum_bank", tag="a0")
        prexp = []
        for k in range(STRIPS):
            top2 = sb("top2_%d" % k, [P, 2, GROUPS], F32)
            top = sb("top%d" % k, [P, GROUPS], F32)
            e = sb("prexp%d" % k, [P, D, GROUPS], F32)
            below = slots[:, k + 1, :].rearrange("p (d g) -> p d g", d=D)
            planes = cosn[k][:].rearrange("p d t v -> p d (t v)")
            nc.vector.tensor_tensor(cosn[k][:], num[:, :, :, k * RUN : (k + 1) * RUN], cosn[k][:], ALU.mult)
            nc.vector.tensor_tensor(top2[:], planes[:, 0:2, :], planes[:, 2:4, :], ALU.max)
            nc.vector.tensor_tensor(top[:], top2[:, 0, :], top2[:, 1, :], ALU.max)
            nc.vector.tensor_tensor(below, planes, top[:].unsqueeze(1).to_broadcast([P, D, GROUPS]), ALU.subtract)
            nc.scalar.activation(e[:], below, ACT.Exp)
            for d in range(D):
                nc.tensor.matmul(
                    sum_bank[:, k, :], lhsT=e[:, d, :], rhs=identity[:], is_transpose=True,
                    start=(d == 0), stop=(d == D - 1),
                )
            prexp.append(e)
        for t in range(PACK):
            nc.scalar.activation(
                unit_dst[:, t, :, :].rearrange("p d v -> p v d"),
                members(dst[:, t, :]),
                ACT.Copy,
                scale=unit_sb[:, t : t + 1],
            )
        for k in range(STRIPS):
            rows = prexp[k][:].rearrange("p d (t v) -> p t d v", t=PACK)
            nc.vector.tensor_tensor(rows, rows, unit_dst[:, :, :, k * RUN : (k + 1) * RUN], ALU.mult)
        for t in range(PACK):
            nc.vector.tensor_scalar(
                unit_vel[:, :, t, :, :].rearrange("p s d v -> p s v d"),
                vel[:, t, :].rearrange("p (s v d) -> p s v d", v=RUN, d=D),
                unit_f[:, t : t + 1],
                None,
                ALU.mult,
            )

        w3_grouped = sb("w3_grouped", [P, N, PACK], BF16)
        nc.gpsimd.tensor_scalar(w3_grouped[:], w3_raw[:].rearrange("p j n -> p n j"), 1.0, 0.0, ALU.mult, ALU.add)
        w3_codes, w3_scale = quantize("w3", w3_grouped[:].rearrange("p n j -> p (n j)"), N)

        inv_root = sb("inv_root", [P, STRIPS, P], F32)
        nc.scalar.activation(inv_root[:], sum_bank[:], ACT.Abs_reciprocal_sqrt)
        inv_sum = []
        for k in range(STRIPS):
            nc.scalar.activation(inv_root[:, k, :], inv_root[:, k, :], ACT.Square)
            bank = psum.tile([P, S], F32, name="inv_sum%d" % k, tag="b%d" % k)
            nc.tensor.transpose(bank[:, 0:GROUPS], inv_root[:, k, :], identity[:])
            inv_sum.append(bank)
        for k in range(STRIPS):
            drift = cosn[k][:].rearrange("p d t v -> p (d t v)")
            hid_grouped = sb("hid_grouped%d" % k, [P, P, PACK], BF16)
            nc.vector.tensor_tensor(
                drift.rearrange("p (t d v) -> p d t v", t=PACK, d=D),
                prexp[k][:].rearrange("p d (t v) -> p d t v", t=PACK),
                inv_sum[k][:, 0:GROUPS].rearrange("p (t v) -> p t v", t=PACK).unsqueeze(1).to_broadcast([P, D, PACK, RUN]),
                ALU.mult,
            )
            nc.vector.tensor_tensor(
                hid_grouped[:].rearrange("p (c i) t -> p c t i", i=4),
                drift.rearrange("p (t c i) -> p c t i", t=PACK, i=4),
                unit_vel[:, k, :, :, :].rearrange("p t d (c i) -> p (d c) t i", i=4),
                ALU.add,
            )
            codes, scale = quantize("hid_%d" % k, hid_grouped[:].rearrange("p j t -> p (j t)"), P)
            bank = psum.tile([P, S], F32, name="out_bank%d" % k, tag="a%d" % ((k + 1) % 4))
            nc.tensor.matmul_mx(
                out=bank[:, 0:P],
                lhsT=w3_codes[:].bitcast(FP8X4),
                lhsT_scale=w3_scale[:],
                rhs=codes[:].bitcast(FP8X4),
                rhs_scale=scale[:],
                start=True,
                stop=True,
            )
            result = sb("result%d" % k, [P, P], F32)
            nc.scalar.copy(out=members(result[:]), in_=bank[:, 0:P].rearrange("m (d v) -> m v d", d=D))
            nc.sync.dma_start(out=out[:, k * P : (k + 1) * P], in_=result[:])
